import numpy as np
import ml_dtypes


def mxq(x, axis, fmt="e4m3"):
    dtype, down = {"e4m3": (ml_dtypes.float8_e4m3fn, 7), "e5m2": (ml_dtypes.float8_e5m2, 14)}[fmt]
    v = np.moveaxis(np.asarray(x, np.float32).astype(ml_dtypes.bfloat16).astype(np.float64), axis, -1)
    blocks = v.reshape(v.shape[:-1] + (-1, 32))
    amax = np.abs(blocks).max(-1, keepdims=True)
    byte = np.maximum(np.where(amax > 0, np.frexp(amax)[1] - 1 + 127, 0) - down, 1)
    scale = np.exp2(byte - 127.0)
    codes = (blocks / scale).astype(np.float32).astype(dtype).astype(np.float64)
    return np.moveaxis((codes * scale).reshape(v.shape), -1, axis)


WIDE = False


def mx_kscale(k):
    if not WIDE:
        return np.ones(k)
    levels = np.array([10, -10, 5, -5, 0])
    if k % 512:
        return np.exp2(np.random.permutation(np.resize(levels, k // 32))).repeat(32)
    a = np.empty((k // 512, 16))
    for p in range(k // 512):
        a[p, :8] = np.random.permutation(np.resize(levels, 8))
        for g in range(8):
            far = levels[np.abs(levels - a[p, g]) >= 10]
            a[p, g + 8] = far[np.random.randint(len(far))]
    return np.exp2(a.ravel()).repeat(32)


def f64(x):
    return np.asarray(x).astype(np.float64)


def striped(idx):
    return np.tile(idx.reshape(-1, 16).T, (8, 1)).astype(np.uint16)


def unstriped(offs):
    return offs[:16].T.reshape(-1).astype(np.int64)


E2M1 = np.array([0.0, 0.5, 1.0, 1.5, 2.0, 3.0, 4.0, 6.0, -0.0, -0.5, -1.0, -1.5, -2.0, -3.0, -4.0, -6.0])


def pack_weight(w, fmt):
    k, n = w.shape
    w = f64(np.asarray(w, np.float32).astype(ml_dtypes.bfloat16)).reshape(k // 32, 32, n)
    amax = np.abs(w).max(1)
    if fmt == "e4m3":
        byte = np.frexp(amax)[1] - 1 + 127 - 7
    else:
        mant, ex = np.frexp(amax / 6.0)
        byte = np.where(mant > 0.5, ex, ex - 1) + 127
    byte = np.clip(np.where(amax > 0, byte, 1), 1, 254)
    scaled = (w * np.exp2(127.0 - byte)[:, None, :]).reshape(k, n).astype(np.float32)
    by_word = np.ascontiguousarray(scaled.reshape(k // 512, 128, 4, n).transpose(0, 1, 3, 2))
    if fmt == "e4m3":
        words = by_word.astype(ml_dtypes.float8_e4m3fn).view(np.uint8)
    else:
        c = by_word.astype(ml_dtypes.float4_e2m1fn).view(np.uint8) & 0xF
        words = (c[..., 0::2] | (c[..., 1::2] << 4)).reshape(k // 512, 128, 2 * n)
    return np.ascontiguousarray(words), np.ascontiguousarray(byte.astype(np.uint8).reshape(k // 512, 16, n))


def unpack_weight(words, scales, fmt):
    g, _, n = scales.shape
    words = np.ascontiguousarray(words).reshape(g, 128, n, -1)
    if fmt == "e4m3":
        vals = words.view(ml_dtypes.float8_e4m3fn).astype(np.float64)
    else:
        nib = np.empty((g, 128, n, 4), np.uint8)
        nib[..., 0::2] = words & 0xF
        nib[..., 1::2] = words >> 4
        vals = E2M1[nib]
    vals = vals * np.repeat(np.exp2(scales.astype(np.float64) - 127.0), 8, axis=1)[..., None]
    return vals.transpose(0, 1, 3, 2).reshape(g * 512, n)


def d_silu(v):
    s = 1.0 / (1.0 + np.exp(-np.maximum(v, -700.0)))
    return s * (1.0 + v * (1.0 - s))


K, T, E, C, H, N = 512, 1280, 5, 256, 512, 1024


def by_expert(wq, xq):
    return np.concatenate([wq[e].T @ xq[:, e * C:(e + 1) * C] for e in range(E)], axis=1)


def setup_inputs():
    n = np.random.standard_normal
    s = mx_kscale(K)
    v = mx_kscale(N)
    u = mx_kscale(H)
    slot_token = np.random.permutation(T)[:E * C]
    w_slot = np.random.uniform(0.2, 1.0, E * C)
    x = pack_weight(n((K, T)) * s[:, None], "e4m3")
    dy = pack_weight(n((N, T)) * v[:, None], "e4m3")
    m1 = n((E, K, H))
    w1 = [pack_weight(m, "e2m1") for m in m1 / np.sqrt(K) / s[None, :, None]]
    w2t = [pack_weight(m, "e2m1") for m in n((E, N, H)) / np.sqrt(N) / v[None, :, None] * u]
    w1t = [pack_weight(m, "e2m1") for m in m1.transpose(0, 2, 1) / np.sqrt(H) / u[None, :, None]]
    return {
        "x_words": x[0],
        "x_scales": x[1],
        "dy_words": dy[0],
        "dy_scales": dy[1],
        "w1_words": np.stack([m[0] for m in w1]),
        "w1_scales": np.stack([m[1] for m in w1]),
        "w2t_words": np.stack([m[0] for m in w2t]),
        "w2t_scales": np.stack([m[1] for m in w2t]),
        "w1t_words": np.stack([m[0] for m in w1t]),
        "w1t_scales": np.stack([m[1] for m in w1t]),
        "gate": (np.tile(w_slot, (128, 1))).astype(np.float32),
        "offs": striped(slot_token),
    }


def reference(x_words, x_scales, dy_words, dy_scales, w1_words, w1_scales, w2t_words, w2t_scales, w1t_words, w1t_scales, gate, offs):
    w1 = np.stack([unpack_weight(w1_words[e], w1_scales[e], "e2m1") for e in range(E)])
    w2t = np.stack([unpack_weight(w2t_words[e], w2t_scales[e], "e2m1") for e in range(E)])
    w1t = np.stack([unpack_weight(w1t_words[e], w1t_scales[e], "e2m1") for e in range(E)])
    idx = unstriped(offs)
    xq = unpack_weight(x_words, x_scales, "e4m3")[:, idx]
    gq = unpack_weight(dy_words, dy_scales, "e4m3")[:, idx]
    dh = f64(gate[:1]) * by_expert(w2t, gq)
    a = by_expert(w1, xq)
    dx = by_expert(w1t, mxq(dh * d_silu(a), 0, "e4m3"))
    out = np.zeros((K, T))
    out[:, idx] = dx
    return out

@@ -1,0 +1,213 @@
+from contextlib import ExitStack
+
+import concourse.mybir as mybir
+from concourse.masks import make_identity
+
+K, T, E, C, H, N = 512, 1280, 5, 256, 512, 1024
+FLOPS = 2 * E * C * H * (K + N + K)
+
+F32 = mybir.dt.float32
+BF16 = mybir.dt.bfloat16
+I32 = mybir.dt.int32
+U32 = mybir.dt.uint32
+U16 = mybir.dt.uint16
+U8 = mybir.dt.uint8
+FP8X4 = mybir.dt.float8_e4m3fn_x4
+FP4X4 = mybir.dt.float4_e2m1fn_x4
+ACT = mybir.ActivationFunctionType
+ALU = mybir.AluOpType
+
+P = 128
+SLOTS = E * C
+BLOCKS = SLOTS // P
+PASSES = N // 512
+GATHER_CUTS = [(0, 512), (512, 1280)]
+SCATTER_CUTS = [(0, 256), (256, 768), (768, 1280)]
+
+
+def tile_moe_rec_mlp_silu_kernel(
+    tc, x_words, x_scales, dy_words, dy_scales, w1_words, w1_scales, w2t_words, w2t_scales,
+    w1t_words, w1t_scales, gate, offs, out,
+):
+    nc = tc.nc
+    with ExitStack() as ctx:
+        held = ctx.enter_context(tc.tile_pool(name="held", bufs=1))
+        work = ctx.enter_context(tc.tile_pool(name="work", bufs=3))
+        psum = ctx.enter_context(tc.psum_pool(name="psum", bufs=2))
+
+        offsets = held.tile([P, SLOTS // 16], U16, name="offsets")
+        nc.sync.dma_start(offsets[:], offs)
+
+        def listed(lo, hi):
+            return offsets[:, lo // 16 : hi // 16]
+
+        def load_words(name, words):
+            win = held.tile([P, T], I32, name=name)
+            nc.sync.dma_start(win[:], words.rearrange("p t d -> p (t d)").bitcast(I32))
+            return win
+
+        def load_planes(name, scales):
+            groups, width = scales.shape[0], scales.shape[2]
+            planes = held.tile([P, groups, width], U8, name=name, align_bytes=64)
+            nc.vector.memset(planes[:].rearrange("p g n -> p (g n)").bitcast(I32), 0)
+            for q in range(4):
+                nc.sync.dma_start(
+                    planes[32 * q : 32 * q + 4, :, :].bitcast(I32),
+                    scales[:, 4 * q : 4 * q + 4, :].rearrange("g r n -> r g n").bitcast(I32),
+                )
+            return planes
+
+        def load_codes(codes, words, e0, e1):
+            per = words.shape[1]
+            nc.sync.dma_start(
+                codes[:, e0 * per : e1 * per, :].bitcast(I32),
+                words[e0:e1].rearrange("e s p n -> p (e s) n").bitcast(I32),
+            )
+
+        w1_codes = held.tile([P, E, 2 * H], U8, name="w1_codes", align_bytes=64)
+        w2_codes = held.tile([P, E * PASSES, 2 * H], U8, name="w2_codes", align_bytes=64)
+        w1t_codes = held.tile([P, E, 2 * K], U8, name="w1t_codes", align_bytes=64)
+        gate_rows = held.tile([P, P], F32, name="gate_rows")
+
+        x_win = load_words("x_win", x_words[0])
+        xs_win = load_planes("xs_win", x_scales)
+        w1_planes = load_planes("w1_planes", w1_scales.rearrange("e s r n -> (e s) r n"))
+        load_codes(w1_codes, w1_words, 0, 2)
+        nc.sync.dma_start(gate_rows[:], gate.rearrange("r (b p) -> (r b) p", p=P)[0:P, :])
+        dy_win = [load_words("dy_win%d" % s, dy_words[s]) for s in range(PASSES)]
+        load_codes(w1_codes, w1_words, 2, E)
+        dys_win = held.tile([P, T], U8, name="dys_win", align_bytes=64)
+        nc.vector.memset(dys_win[:].bitcast(I32), 0)
+        for q in range(4):
+            nc.sync.dma_start(
+                dys_win[32 * q : 32 * q + 4 * PASSES, :].bitcast(I32),
+                dy_scales[:, 4 * q : 4 * q + 4, :].bitcast(I32),
+            )
+        w2_planes = load_planes("w2_planes", w2t_scales.rearrange("e s r n -> (e s) r n"))
+        load_codes(w2_codes, w2t_words, 0, 2)
+        w1t_planes = load_planes("w1t_planes", w1t_scales.rearrange("e s r n -> (e s) r n"))
+        load_codes(w2_codes, w2t_words, 2, E)
+        load_codes(w1t_codes, w1t_words, 0, E)
+
+        ident = held.tile([P, P], F32, name="ident")
+        make_identity(nc, ident[:])
+        gate_ps = psum.tile([P, 2, 2, P], F32, name="turned", tag="turned")
+        nc.tensor.transpose(gate_ps[:, 0, 0, :], gate_rows[:], ident[:])
+        half_gate = held.tile([P, BLOCKS], F32, name="half_gate")
+        neg_half_gate = held.tile([P, BLOCKS], F32, name="neg_half_gate")
+        nc.scalar.activation(half_gate[:], gate_ps[:, 0, 0, 0:BLOCKS], ACT.Copy, scale=0.5)
+        nc.scalar.activation(neg_half_gate[:], gate_ps[:, 0, 0, 0:BLOCKS], ACT.Copy, scale=-0.5)
+
+        def gather(name, window, dtype, cut):
+            lo, hi = cut
+            got = held.tile([P, hi - lo], dtype, name="%s_%d" % (name, lo), align_bytes=64)
+            nc.vector.tensor_copy(got[:], window.indirect(listed(lo, hi)))
+            return got
+
+        def cut_of(block):
+            c = max(i for i, cut in enumerate(GATHER_CUTS) if cut[0] <= block * P)
+            lo = GATHER_CUTS[c][0]
+            return c, slice(block * P - lo, (block + 1) * P - lo)
+
+        x_got, xs_got, dy_got, dys_got = [], [], [], []
+        for cut in GATHER_CUTS:
+            x_got.append(gather("x_got", x_win[:].bitcast(U32), U32, cut))
+            xs_got.append(gather("xs_got", xs_win[:, 0, :], U8, cut))
+
+        def gather_dy(cut):
+            both = gather("dys_got", dys_win[:], U8, cut)
+            moved = held.tile([P, cut[1] - cut[0]], U8, name="dys_moved%d" % cut[0], align_bytes=64)
+            nc.vector.memset(moved[:].bitcast(I32), 0)
+            nc.sync.dma_start(moved[0:112, :].bitcast(I32), both[4:116, :].bitcast(I32))
+            dys_got.append([both, moved])
+            dy_got.append([gather("dy_got%d" % s, dy_win[s][:].bitcast(U32), U32, cut) for s in range(PASSES)])
+
+        th, gated = {}, {}
+
+        def recompute(block):
+            e = block * P // C
+            c, cols = cut_of(block)
+            a_ps = psum.tile([P, H], F32, name="a_ps")
+            nc.tensor.matmul_mx(
+                out=a_ps[:], lhsT=x_got[c][:, cols].bitcast(FP8X4), lhsT_scale=xs_got[c][:, cols],
+                rhs=w1_codes[:, e, :].bitcast(FP4X4), rhs_scale=w1_planes[:, e, :], start=True, stop=True,
+            )
+            neg_silu = work.tile([P, H], F32, name="neg_silu")
+            nc.scalar.activation(neg_silu[:], a_ps[:], ACT.Silu, scale=-1.0)
+            th[block] = held.tile([P, H], F32, name="th%d" % block)
+            nc.scalar.activation(th[block][:], a_ps[:], ACT.Tanh, scale=0.5)
+            gated[block] = held.tile([P, H], F32, name="gated%d" % block)
+            nc.scalar.activation(
+                gated[block][:], neg_silu[:], ACT.Identity,
+                bias=half_gate[:, block : block + 1], scale=neg_half_gate[:, block : block + 1],
+            )
+
+        results = {}
+        for lo, hi in SCATTER_CUTS:
+            results[lo] = held.tile([P, K // P, hi - lo], F32, name="dx_%d" % lo)
+
+        da_mx = {}
+
+        def front(e):
+            turned = psum.tile([P, 2, 2, P], F32, name="turned", tag="turned")
+            for b in range(C // P):
+                block = e * (C // P) + b
+                c, cols = cut_of(block)
+                slope = held.tile([P, H], F32, name="slope%d" % block)
+                nc.vector.scalar_tensor_tensor(slope[:], th[block][:], 1.0, gated[block][:], ALU.add, ALU.mult)
+                dh_ps = psum.tile([P, H], F32, name="dh_ps")
+                for s in range(PASSES):
+                    g = e * PASSES + s
+                    nc.tensor.matmul_mx(
+                        out=dh_ps[:], lhsT=dy_got[c][s][:, cols].bitcast(FP8X4), lhsT_scale=dys_got[c][s][:, cols],
+                        rhs=w2_codes[:, g, :].bitcast(FP4X4), rhs_scale=w2_planes[:, g, :],
+                        start=(s == 0), stop=(s == PASSES - 1),
+                    )
+                da = held.tile([P, H], BF16, name="da%d" % block)
+                nc.vector.tensor_tensor(da[:], dh_ps[:], slope[:], ALU.mult)
+                da_words = da[:].bitcast(F32)
+                for u in range(2):
+                    nc.tensor.transpose(turned[:, b, u, :], da_words[:, u : H // 2 : 2], ident[:])
+            grouped = held.tile([P, 4 * C], BF16, name="grouped%d" % e, align_bytes=64)
+            nc.scalar.copy(
+                grouped[:].bitcast(F32).rearrange("p (b r u) -> p b r u", b=2, u=2),
+                turned[:].rearrange("p b u r -> p b r u"),
+            )
+            da_codes = held.tile([P, C], U32, name="da_codes%d" % e, align_bytes=64)
+            da_scales = held.tile([P, C], U8, name="da_scales%d" % e, align_bytes=64)
+            nc.vector.quantize_mx(out=da_codes[:].bitcast(FP8X4), scales=da_scales[:], in_=grouped[:])
+            da_mx[e] = (da_codes, da_scales)
+
+        def back(e):
+            da_codes, da_scales = da_mx[e]
+            lo = max(start for start in results if start <= e * C)
+            for half in range(2):
+                dx_ps = psum.tile([P, 2, C], F32, name="dx_ps")
+                for j in range(2):
+                    kb = 2 * half + j
+                    nc.tensor.matmul_mx(
+                        out=dx_ps[:, j, :],
+                        lhsT=w1t_codes[:, e, 2 * P * kb : 2 * P * (kb + 1)].bitcast(FP4X4),
+                        lhsT_scale=w1t_planes[:, e, P * kb : P * (kb + 1)],
+                        rhs=da_codes[:].bitcast(FP8X4), rhs_scale=da_scales[:], start=True, stop=True,
+                    )
+                nc.scalar.copy(results[lo][:, 2 * half : 2 * half + 2, e * C - lo : (e + 1) * C - lo], dx_ps[:])
+
+        for cut in GATHER_CUTS:
+            gather_dy(cut)
+        for block in range(BLOCKS - 2):
+            recompute(block)
+        front(0)
+        for block in range(BLOCKS - 2, BLOCKS):
+            recompute(block)
+        for e in range(1, E):
+            front(e)
+        for e in range(E):
+            back(e)
+
+        out_win = [held.tile([P, T], F32, name="out_win%d" % kb) for kb in range(K // P)]
+        for lo, hi in SCATTER_CUTS:
+            for kb in range(K // P):
+                nc.vector.tensor_copy(out_win[kb][:].indirect(listed(lo, hi)), results[lo][:, kb, :])
+        for kb in range(K // P):
+            nc.sync.dma_start(out[kb * P : (kb + 1) * P, :], out_win[kb][:])

@@ -21,8 +21,10 @@ P = 128
 SLOTS = E * C
 BLOCKS = SLOTS // P
 PASSES = N // 512
-GATHER_CUTS = [(0, 512), (512, 1280)]
-SCATTER_CUTS = [(0, 256), (256, 768), (768, 1280)]
+X_CUTS = [(0, 512), (512, 1280)]
+DYS_CUTS = [(0, 512), (512, 1280)]
+DY_CUTS = [(0, 512), (512, 768), (768, 1280)]
+SCATTER_CUTS = [(0, 256), (256, 512), (512, 768), (768, 1024), (1024, 1280)]
 
 
 def tile_moe_rec_mlp_silu_kernel(
@@ -32,7 +34,7 @@ def tile_moe_rec_mlp_silu_kernel(
     nc = tc.nc
     with ExitStack() as ctx:
         held = ctx.enter_context(tc.tile_pool(name="held", bufs=1))
-        work = ctx.enter_context(tc.tile_pool(name="work", bufs=3))
+        work = ctx.enter_context(tc.tile_pool(name="work", bufs=4))
         psum = ctx.enter_context(tc.psum_pool(name="psum", bufs=2))
 
         offsets = held.tile([P, SLOTS // 16], U16, name="offsets")
@@ -46,12 +48,12 @@ def tile_moe_rec_mlp_silu_kernel(
             nc.sync.dma_start(win[:], words.rearrange("p t d -> p (t d)").bitcast(I32))
             return win
 
-        def load_planes(name, scales):
+        def load_planes(name, scales, queue):
             groups, width = scales.shape[0], scales.shape[2]
             planes = held.tile([P, groups, width], U8, name=name, align_bytes=64)
             nc.vector.memset(planes[:].rearrange("p g n -> p (g n)").bitcast(I32), 0)
             for q in range(4):
-                nc.sync.dma_start(
+                queue.dma_start(
                     planes[32 * q : 32 * q + 4, :, :].bitcast(I32),
                     scales[:, 4 * q : 4 * q + 4, :].rearrange("g r n -> r g n").bitcast(I32),
                 )
@@ -68,65 +70,76 @@ def tile_moe_rec_mlp_silu_kernel(
         w2_codes = held.tile([P, E * PASSES, 2 * H], U8, name="w2_codes", align_bytes=64)
         w1t_codes = held.tile([P, E, 2 * K], U8, name="w1t_codes", align_bytes=64)
         gate_rows = held.tile([P, P], F32, name="gate_rows")
-
-        x_win = load_words("x_win", x_words[0])
-        xs_win = load_planes("xs_win", x_scales)
-        w1_planes = load_planes("w1_planes", w1_scales.rearrange("e s r n -> (e s) r n"))
-        load_codes(w1_codes, w1_words, 0, 2)
-        nc.sync.dma_start(gate_rows[:], gate.rearrange("r (b p) -> (r b) p", p=P)[0:P, :])
-        dy_win = [load_words("dy_win%d" % s, dy_words[s]) for s in range(PASSES)]
-        load_codes(w1_codes, w1_words, 2, E)
         dys_win = held.tile([P, T], U8, name="dys_win", align_bytes=64)
-        nc.vector.memset(dys_win[:].bitcast(I32), 0)
-        for q in range(4):
-            nc.sync.dma_start(
-                dys_win[32 * q : 32 * q + 4 * PASSES, :].bitcast(I32),
-                dy_scales[:, 4 * q : 4 * q + 4, :].bitcast(I32),
-            )
-        w2_planes = load_planes("w2_planes", w2t_scales.rearrange("e s r n -> (e s) r n"))
+
+        def load_dys(queue):
+            nc.vector.memset(dys_win[:].bitcast(I32), 0)
+            for q in range(4):
+                queue.dma_start(
+                    dys_win[32 * q : 32 * q + 4 * PASSES, :].bitcast(I32),
+                    dy_scales[:, 4 * q : 4 * q + 4, :].bitcast(I32),
+                )
+
+        xs_win = load_planes("xs_win", x_scales, nc.scalar)
+        x_win = load_words("x_win", x_words[0])
+        load_codes(w1_codes, w1_words, 0, 2)
+        w1_planes = load_planes("w1_planes", w1_scales.rearrange("e s r n -> (e s) r n"), nc.scalar)
+        nc.sync.dma_start(gate_rows[:], gate.rearrange("r (b p) -> (r b) p", p=P)[0:P, :])
+        load_dys(nc.sync)
+        dy_both = held.tile([P, PASSES, T], I32, name="dy_both")
+        nc.sync.dma_start(dy_both[:], dy_words.rearrange("s p t d -> p s (t d)").bitcast(I32))
+        dy_win = [dy_both[:, s, :] for s in range(PASSES)]
+        load_codes(w1_codes, w1_words, 2, E)
+        w2_planes = load_planes("w2_planes", w2t_scales.rearrange("e s r n -> (e s) r n"), nc.sync)
         load_codes(w2_codes, w2t_words, 0, 2)
-        w1t_planes = load_planes("w1t_planes", w1t_scales.rearrange("e s r n -> (e s) r n"))
-        load_codes(w2_codes, w2t_words, 2, E)
-        load_codes(w1t_codes, w1t_words, 0, E)
 
         ident = held.tile([P, P], F32, name="ident")
         make_identity(nc, ident[:])
-        gate_ps = psum.tile([P, 2, 2, P], F32, name="turned", tag="turned")
+        gate_ps = psum.tile([P, 2, 2, P], F32, name="turned", tag="turned", bufs=2)
         nc.tensor.transpose(gate_ps[:, 0, 0, :], gate_rows[:], ident[:])
         half_gate = held.tile([P, BLOCKS], F32, name="half_gate")
         neg_half_gate = held.tile([P, BLOCKS], F32, name="neg_half_gate")
         nc.scalar.activation(half_gate[:], gate_ps[:, 0, 0, 0:BLOCKS], ACT.Copy, scale=0.5)
         nc.scalar.activation(neg_half_gate[:], gate_ps[:, 0, 0, 0:BLOCKS], ACT.Copy, scale=-0.5)
 
-        def gather(name, window, dtype, cut):
+        def gather(name, window, dtype, cut, tag=""):
             lo, hi = cut
-            got = held.tile([P, hi - lo], dtype, name="%s_%d" % (name, lo), align_bytes=64)
+            got = held.tile([P, hi - lo], dtype, name="%s_%d" % (name, lo), tag=tag, align_bytes=64)
             nc.vector.tensor_copy(got[:], window.indirect(listed(lo, hi)))
             return got
 
-        def cut_of(block):
-            c = max(i for i, cut in enumerate(GATHER_CUTS) if cut[0] <= block * P)
-            lo = GATHER_CUTS[c][0]
+        def cut_of(cuts, block):
+            c = max(i for i, cut in enumerate(cuts) if cut[0] <= block * P)
+            lo = cuts[c][0]
             return c, slice(block * P - lo, (block + 1) * P - lo)
 
-        x_got, xs_got, dy_got, dys_got = [], [], [], []
-        for cut in GATHER_CUTS:
-            x_got.append(gather("x_got", x_win[:].bitcast(U32), U32, cut))
+        x_got, xs_got, dy_got, dys_got = [], [], [{}, {}], []
+        for cut in X_CUTS:
             xs_got.append(gather("xs_got", xs_win[:, 0, :], U8, cut))
-
-        def gather_dy(cut):
+            x_got.append(gather("x_got", x_win[:].bitcast(U32), U32, cut))
+        for cut in DYS_CUTS:
             both = gather("dys_got", dys_win[:], U8, cut)
             moved = held.tile([P, cut[1] - cut[0]], U8, name="dys_moved%d" % cut[0], align_bytes=64)
             nc.vector.memset(moved[:].bitcast(I32), 0)
             nc.sync.dma_start(moved[0:112, :].bitcast(I32), both[4:116, :].bitcast(I32))
             dys_got.append([both, moved])
-            dy_got.append([gather("dy_got%d" % s, dy_win[s][:].bitcast(U32), U32, cut) for s in range(PASSES)])
 
-        th, gated = {}, {}
+        def gather_dy(s, cut, tag=""):
+            dy_got[s][cut[0]] = gather("dy_got%d" % s, dy_win[s][:].bitcast(U32), U32, cut, tag)
+
+        for cut in DY_CUTS[:2]:
+            for s in range(PASSES):
+                gather_dy(s, cut)
+
+        load_codes(w2_codes, w2t_words, 2, E)
+        w1t_planes = load_planes("w1t_planes", w1t_scales.rearrange("e s r n -> (e s) r n"), nc.sync)
+        load_codes(w1t_codes, w1t_words, 0, E)
+
+        slopes, grouped, da_mx, turned = {}, {}, {}, {}
 
         def recompute(block):
             e = block * P // C
-            c, cols = cut_of(block)
+            c, cols = cut_of(X_CUTS, block)
             a_ps = psum.tile([P, H], F32, name="a_ps")
             nc.tensor.matmul_mx(
                 out=a_ps[:], lhsT=x_got[c][:, cols].bitcast(FP8X4), lhsT_scale=xs_got[c][:, cols],
@@ -134,55 +147,59 @@ def tile_moe_rec_mlp_silu_kernel(
             )
             neg_silu = work.tile([P, H], F32, name="neg_silu")
             nc.scalar.activation(neg_silu[:], a_ps[:], ACT.Silu, scale=-1.0)
-            th[block] = held.tile([P, H], F32, name="th%d" % block)
-            nc.scalar.activation(th[block][:], a_ps[:], ACT.Tanh, scale=0.5)
-            gated[block] = held.tile([P, H], F32, name="gated%d" % block)
+            th = work.tile([P, H], F32, name="th")
+            nc.scalar.activation(th[:], a_ps[:], ACT.Tanh, scale=0.5)
+            gated = work.tile([P, H], F32, name="gated")
             nc.scalar.activation(
-                gated[block][:], neg_silu[:], ACT.Identity,
+                gated[:], neg_silu[:], ACT.Identity,
                 bias=half_gate[:, block : block + 1], scale=neg_half_gate[:, block : block + 1],
             )
+            slope = held.tile([P, H], F32, name="slope%d" % block, align_bytes=64)
+            nc.vector.scalar_tensor_tensor(slope[:], th[:], 1.0, gated[:], ALU.add, ALU.mult)
+            slopes[block] = slope
+
+        def hidden_gradient(block):
+            e, b = divmod(block, C // P)
+            c, cols = cut_of(DY_CUTS, block)
+            cs, scale_cols = cut_of(DYS_CUTS, block)
+            dh_ps = psum.tile([P, H], F32, name="dh_ps", bufs=4)
+            for s in range(PASSES):
+                g = e * PASSES + s
+                nc.tensor.matmul_mx(
+                    out=dh_ps[:], lhsT=dy_got[s][DY_CUTS[c][0]][:, cols].bitcast(FP8X4), lhsT_scale=dys_got[cs][s][:, scale_cols],
+                    rhs=w2_codes[:, g, :].bitcast(FP4X4), rhs_scale=w2_planes[:, g, :],
+                    start=(s == 0), stop=(s == PASSES - 1),
+                )
+            da = held.tile([P, H], BF16, name="da%d" % block)
+            nc.vector.tensor_tensor(da[:], dh_ps[:], slopes[block][:], ALU.mult)
+            da_words = da[:].bitcast(F32)
+            if b == 0:
+                turned[e] = psum.tile([P, 2, 2, P], F32, name="turned", tag="turned", bufs=2)
+            for u in range(2):
+                nc.tensor.transpose(turned[e][:, b, u, :], da_words[:, u : H // 2 : 2], ident[:])
+            if b == 1:
+                grouped[e] = held.tile([P, 4 * C], BF16, name="grouped%d" % e, align_bytes=64)
+                nc.scalar.copy(
+                    grouped[e][:].bitcast(F32).rearrange("p (b r u) -> p b r u", b=2, u=2),
+                    turned[e][:].rearrange("p b u r -> p b r u"),
+                )
+
+        def quantise(e):
+            tag = "slope%d" % min(2 * e + 3, BLOCKS - 1) if e < E - 1 else "last_codes"
+            da_codes = held.tile([P, C], U32, name="da_codes%d" % e, tag=tag, align_bytes=64)
+            da_scales = held.tile([P, C], U8, name="da_scales%d" % e, align_bytes=64)
+            nc.vector.quantize_mx(out=da_codes[:].bitcast(FP8X4), scales=da_scales[:], in_=grouped[e][:])
+            da_mx[e] = (da_codes, da_scales)
 
         results = {}
         for lo, hi in SCATTER_CUTS:
             results[lo] = held.tile([P, K // P, hi - lo], F32, name="dx_%d" % lo)
 
-        da_mx = {}
-
-        def front(e):
-            turned = psum.tile([P, 2, 2, P], F32, name="turned", tag="turned")
-            for b in range(C // P):
-                block = e * (C // P) + b
-                c, cols = cut_of(block)
-                slope = held.tile([P, H], F32, name="slope%d" % block)
-                nc.vector.scalar_tensor_tensor(slope[:], th[block][:], 1.0, gated[block][:], ALU.add, ALU.mult)
-                dh_ps = psum.tile([P, H], F32, name="dh_ps")
-                for s in range(PASSES):
-                    g = e * PASSES + s
-                    nc.tensor.matmul_mx(
-                        out=dh_ps[:], lhsT=dy_got[c][s][:, cols].bitcast(FP8X4), lhsT_scale=dys_got[c][s][:, cols],
-                        rhs=w2_codes[:, g, :].bitcast(FP4X4), rhs_scale=w2_planes[:, g, :],
-                        start=(s == 0), stop=(s == PASSES - 1),
-                    )
-                da = held.tile([P, H], BF16, name="da%d" % block)
-                nc.vector.tensor_tensor(da[:], dh_ps[:], slope[:], ALU.mult)
-                da_words = da[:].bitcast(F32)
-                for u in range(2):
-                    nc.tensor.transpose(turned[:, b, u, :], da_words[:, u : H // 2 : 2], ident[:])
-            grouped = held.tile([P, 4 * C], BF16, name="grouped%d" % e, align_bytes=64)
-            nc.scalar.copy(
-                grouped[:].bitcast(F32).rearrange("p (b r u) -> p b r u", b=2, u=2),
-                turned[:].rearrange("p b u r -> p b r u"),
-            )
-            da_codes = held.tile([P, C], U32, name="da_codes%d" % e, align_bytes=64)
-            da_scales = held.tile([P, C], U8, name="da_scales%d" % e, align_bytes=64)
-            nc.vector.quantize_mx(out=da_codes[:].bitcast(FP8X4), scales=da_scales[:], in_=grouped[:])
-            da_mx[e] = (da_codes, da_scales)
-
-        def back(e):
+        def input_gradient(e):
             da_codes, da_scales = da_mx[e]
             lo = max(start for start in results if start <= e * C)
             for half in range(2):
-                dx_ps = psum.tile([P, 2, C], F32, name="dx_ps")
+                dx_ps = psum.tile([P, 2, C], F32, name="dx_ps", tag="a_ps")
                 for j in range(2):
                     kb = 2 * half + j
                     nc.tensor.matmul_mx(
@@ -193,19 +210,23 @@ def tile_moe_rec_mlp_silu_kernel(
                     )
                 nc.scalar.copy(results[lo][:, 2 * half : 2 * half + 2, e * C - lo : (e + 1) * C - lo], dx_ps[:])
 
-        for cut in GATHER_CUTS:
-            gather_dy(cut)
-        for block in range(BLOCKS - 2):
+        for block in range(BLOCKS):
             recompute(block)
-        front(0)
-        for block in range(BLOCKS - 2, BLOCKS):
-            recompute(block)
-        for e in range(1, E):
-            front(e)
+        hidden_gradient(0)
+        gather_dy(0, DY_CUTS[2], "slope0")
+        hidden_gradient(1)
+        hidden_gradient(2)
+        gather_dy(1, DY_CUTS[2], "slope2")
+        hidden_gradient(3)
         for e in range(E):
-            back(e)
+            quantise(e)
+            input_gradient(e)
+            for block in range(2 * e + 4, min(2 * e + 6, BLOCKS)):
+                hidden_gradient(block)
 
-        out_win = [held.tile([P, T], F32, name="out_win%d" % kb) for kb in range(K // P)]
+        out_win = [
+            held.tile([P, T], F32, name="out_win%d" % kb, tag=["w0", "grouped1", "grouped2", "grouped4"][kb], align_bytes=64) for kb in range(K // P)
+        ]
         for lo, hi in SCATTER_CUTS:
             for kb in range(K // P):
                 nc.vector.tensor_copy(out_win[kb][:].indirect(listed(lo, hi)), results[lo][:, kb, :])

@@ -22,6 +22,10 @@ SLOTS = E * C
 BLOCKS = SLOTS // P
 PASSES = N // 512
 X_CUTS = [(0, 512), (512, 1280)]
+TAGS = {'win1': 'grouped3', 'codes3': 'slope9', 'dy12': 'slope3', 'win0': 'slope4'}
+DB, TB, AB, XB = (4, 1, 2, 1)
+SLOPE_ON = "VVSSVVVGSS"
+DA_ON = "VVVVVVGGGG"
 DYS_CUTS = [(0, 512), (512, 1280)]
 DY_CUTS = [(0, 512), (512, 768), (768, 1280)]
 SCATTER_CUTS = [(0, 256), (256, 512), (512, 768), (768, 1024), (1024, 1280)]
@@ -34,7 +38,7 @@ def tile_moe_rec_mlp_silu_kernel(
     nc = tc.nc
     with ExitStack() as ctx:
         held = ctx.enter_context(tc.tile_pool(name="held", bufs=1))
-        work = ctx.enter_context(tc.tile_pool(name="work", bufs=4))
+        work = ctx.enter_context(tc.tile_pool(name="work", bufs=6))
         psum = ctx.enter_context(tc.psum_pool(name="psum", bufs=2))
 
         offsets = held.tile([P, SLOTS // 16], U16, name="offsets")
@@ -95,7 +99,7 @@ def tile_moe_rec_mlp_silu_kernel(
 
         ident = held.tile([P, P], F32, name="ident")
         make_identity(nc, ident[:])
-        gate_ps = psum.tile([P, 2, 2, P], F32, name="turned", tag="turned", bufs=2)
+        gate_ps = psum.tile([P, 2, 2, P], F32, name="turned", tag="turned", bufs=TB)
         nc.tensor.transpose(gate_ps[:, 0, 0, :], gate_rows[:], ident[:])
         half_gate = held.tile([P, BLOCKS], F32, name="half_gate")
         neg_half_gate = held.tile([P, BLOCKS], F32, name="neg_half_gate")
@@ -113,56 +117,72 @@ def tile_moe_rec_mlp_silu_kernel(
             lo = cuts[c][0]
             return c, slice(block * P - lo, (block + 1) * P - lo)
 
-        x_got, xs_got, dy_got, dys_got = [], [], [{}, {}], []
-        for cut in X_CUTS:
-            xs_got.append(gather("xs_got", xs_win[:, 0, :], U8, cut))
-            x_got.append(gather("x_got", x_win[:].bitcast(U32), U32, cut))
-        for cut in DYS_CUTS:
-            both = gather("dys_got", dys_win[:], U8, cut)
+        x_got, xs_got, dy_got, dys_got = {}, {}, [{}, {}], {}
+
+        def gather_x(c):
+            x_got[c] = gather("x_got", x_win[:].bitcast(U32), U32, X_CUTS[c], TAGS.get("x%d" % c, ""))
+
+        def gather_xs(c):
+            xs_got[c] = gather("xs_got", xs_win[:, 0, :], U8, X_CUTS[c], TAGS.get("xs%d" % c, ""))
+
+        def gather_dys(c):
+            cut = DYS_CUTS[c]
+            both = gather("dys_got", dys_win[:], U8, cut, TAGS.get("dys%d" % c, ""))
             moved = held.tile([P, cut[1] - cut[0]], U8, name="dys_moved%d" % cut[0], align_bytes=64)
             nc.vector.memset(moved[:].bitcast(I32), 0)
             nc.sync.dma_start(moved[0:112, :].bitcast(I32), both[4:116, :].bitcast(I32))
-            dys_got.append([both, moved])
+            dys_got[c] = [both, moved]
 
-        def gather_dy(s, cut, tag=""):
-            dy_got[s][cut[0]] = gather("dy_got%d" % s, dy_win[s][:].bitcast(U32), U32, cut, tag)
+        def gather_dy(s, c):
+            cut = DY_CUTS[c]
+            dy_got[s][cut[0]] = gather("dy_got%d" % s, dy_win[s][:].bitcast(U32), U32, cut, TAGS.get("dy%d%d" % (s, c), ""))
 
-        for cut in DY_CUTS[:2]:
-            for s in range(PASSES):
-                gather_dy(s, cut)
+        late = {}
 
-        load_codes(w2_codes, w2t_words, 2, E)
-        w1t_planes = load_planes("w1t_planes", w1t_scales.rearrange("e s r n -> (e s) r n"), nc.sync)
-        load_codes(w1t_codes, w1t_words, 0, E)
+        def load_late(what):
+            if what == 0:
+                load_codes(w2_codes, w2t_words, 2, E)
+            elif what == 1:
+                late["w1t_planes"] = load_planes("w1t_planes", w1t_scales.rearrange("e s r n -> (e s) r n"), nc.sync)
+            else:
+                load_codes(w1t_codes, w1t_words, 0, E)
 
         slopes, grouped, da_mx, turned = {}, {}, {}, {}
 
         def recompute(block):
             e = block * P // C
             c, cols = cut_of(X_CUTS, block)
-            a_ps = psum.tile([P, H], F32, name="a_ps")
+            a_ps = psum.tile([P, H], F32, name="a_ps", bufs=AB)
             nc.tensor.matmul_mx(
                 out=a_ps[:], lhsT=x_got[c][:, cols].bitcast(FP8X4), lhsT_scale=xs_got[c][:, cols],
                 rhs=w1_codes[:, e, :].bitcast(FP4X4), rhs_scale=w1_planes[:, e, :], start=True, stop=True,
             )
             neg_silu = work.tile([P, H], F32, name="neg_silu")
             nc.scalar.activation(neg_silu[:], a_ps[:], ACT.Silu, scale=-1.0)
-            th = work.tile([P, H], F32, name="th")
+            th = held.tile([P, H], F32, name="th%d" % block, align_bytes=64)
             nc.scalar.activation(th[:], a_ps[:], ACT.Tanh, scale=0.5)
-            gated = work.tile([P, H], F32, name="gated")
+            gated = held.tile([P, H], F32, name="gated%d" % block, align_bytes=64)
             nc.scalar.activation(
                 gated[:], neg_silu[:], ACT.Identity,
                 bias=half_gate[:, block : block + 1], scale=neg_half_gate[:, block : block + 1],
             )
             slope = held.tile([P, H], F32, name="slope%d" % block, align_bytes=64)
-            nc.vector.scalar_tensor_tensor(slope[:], th[:], 1.0, gated[:], ALU.add, ALU.mult)
+            if SLOPE_ON[block] == "V":
+                nc.vector.scalar_tensor_tensor(slope[:], th[:], 1.0, gated[:], ALU.add, ALU.mult)
+            else:
+                twice_sg = work.tile([P, H], F32, name="twice_sg")
+                if SLOPE_ON[block] == "S":
+                    nc.scalar.activation(twice_sg[:], th[:], ACT.Identity, bias=1.0)
+                else:
+                    nc.gpsimd.tensor_scalar(twice_sg[:], th[:], 1.0, 1.0, ALU.mult, ALU.add)
+                nc.gpsimd.tensor_tensor(slope[:], twice_sg[:], gated[:], ALU.mult)
             slopes[block] = slope
 
         def hidden_gradient(block):
             e, b = divmod(block, C // P)
             c, cols = cut_of(DY_CUTS, block)
             cs, scale_cols = cut_of(DYS_CUTS, block)
-            dh_ps = psum.tile([P, H], F32, name="dh_ps", bufs=4)
+            dh_ps = psum.tile([P, H], F32, name="dh_ps", bufs=DB)
             for s in range(PASSES):
                 g = e * PASSES + s
                 nc.tensor.matmul_mx(
@@ -171,10 +191,15 @@ def tile_moe_rec_mlp_silu_kernel(
                     start=(s == 0), stop=(s == PASSES - 1),
                 )
             da = held.tile([P, H], BF16, name="da%d" % block)
-            nc.vector.tensor_tensor(da[:], dh_ps[:], slopes[block][:], ALU.mult)
+            if DA_ON[block] == "V":
+                nc.vector.tensor_tensor(da[:], dh_ps[:], slopes[block][:], ALU.mult)
+            else:
+                dh = work.tile([P, H], F32, name="dh")
+                nc.scalar.copy(dh[:], dh_ps[:])
+                nc.gpsimd.tensor_tensor(da[:], dh[:], slopes[block][:], ALU.mult)
             da_words = da[:].bitcast(F32)
             if b == 0:
-                turned[e] = psum.tile([P, 2, 2, P], F32, name="turned", tag="turned", bufs=2)
+                turned[e] = psum.tile([P, 2, 2, P], F32, name="turned", tag="turned", bufs=TB)
             for u in range(2):
                 nc.tensor.transpose(turned[e][:, b, u, :], da_words[:, u : H // 2 : 2], ident[:])
             if b == 1:
@@ -185,7 +210,7 @@ def tile_moe_rec_mlp_silu_kernel(
                 )
 
         def quantise(e):
-            tag = "slope%d" % min(2 * e + 3, BLOCKS - 1) if e < E - 1 else "last_codes"
+            tag = TAGS.get("codes%d" % e, "codes%d" % e)
             da_codes = held.tile([P, C], U32, name="da_codes%d" % e, tag=tag, align_bytes=64)
             da_scales = held.tile([P, C], U8, name="da_scales%d" % e, align_bytes=64)
             nc.vector.quantize_mx(out=da_codes[:].bitcast(FP8X4), scales=da_scales[:], in_=grouped[e][:])
@@ -199,33 +224,65 @@ def tile_moe_rec_mlp_silu_kernel(
             da_codes, da_scales = da_mx[e]
             lo = max(start for start in results if start <= e * C)
             for half in range(2):
-                dx_ps = psum.tile([P, 2, C], F32, name="dx_ps", tag="a_ps")
+                dx_ps = psum.tile([P, 2, C], F32, name="dx_ps", bufs=XB)
                 for j in range(2):
                     kb = 2 * half + j
                     nc.tensor.matmul_mx(
                         out=dx_ps[:, j, :],
                         lhsT=w1t_codes[:, e, 2 * P * kb : 2 * P * (kb + 1)].bitcast(FP4X4),
-                        lhsT_scale=w1t_planes[:, e, P * kb : P * (kb + 1)],
+                        lhsT_scale=late["w1t_planes"][:, e, P * kb : P * (kb + 1)],
                         rhs=da_codes[:].bitcast(FP8X4), rhs_scale=da_scales[:], start=True, stop=True,
                     )
                 nc.scalar.copy(results[lo][:, 2 * half : 2 * half + 2, e * C - lo : (e + 1) * C - lo], dx_ps[:])
 
-        for block in range(BLOCKS):
-            recompute(block)
+        gather_x(0)
+        gather_xs(0)
+        load_late(0)
+        gather_dy(0, 0)
+        gather_dys(0)
+        gather_dy(1, 1)
+        recompute(0)
+        gather_dy(1, 0)
+        gather_xs(1)
+        gather_x(1)
+        recompute(1)
+        recompute(2)
         hidden_gradient(0)
-        gather_dy(0, DY_CUTS[2], "slope0")
         hidden_gradient(1)
+        load_late(2)
         hidden_gradient(2)
-        gather_dy(1, DY_CUTS[2], "slope2")
+        gather_dy(0, 2)
+        load_late(1)
+        quantise(0)
+        gather_dys(1)
+        recompute(3)
+        recompute(4)
+        gather_dy(0, 1)
         hidden_gradient(3)
-        for e in range(E):
-            quantise(e)
-            input_gradient(e)
-            for block in range(2 * e + 4, min(2 * e + 6, BLOCKS)):
-                hidden_gradient(block)
+        input_gradient(0)
+        quantise(1)
+        hidden_gradient(4)
+        recompute(5)
+        recompute(6)
+        input_gradient(1)
+        recompute(7)
+        hidden_gradient(5)
+        recompute(8)
+        recompute(9)
+        gather_dy(1, 2)
+        hidden_gradient(6)
+        hidden_gradient(7)
+        hidden_gradient(8)
+        hidden_gradient(9)
+        quantise(3)
+        quantise(2)
+        input_gradient(2)
+        quantise(4)
+        input_gradient(3)
+        input_gradient(4)
 
         out_win = [
-            held.tile([P, T], F32, name="out_win%d" % kb, tag=["w0", "grouped1", "grouped2", "grouped4"][kb], align_bytes=64) for kb in range(K // P)
+            held.tile([P, T], F32, name="out_win%d" % kb, tag=TAGS.get("win%d" % kb, "win%d" % kb), align_bytes=64) for kb in range(K // P)
         ]
         for lo, hi in SCATTER_CUTS:
             for kb in range(K // P):

@@ -21,13 +21,15 @@ P = 128
 SLOTS = E * C
 BLOCKS = SLOTS // P
 PASSES = N // 512
-X_CUTS = [(0, 512), (512, 1280)]
-TAGS = {'win1': 'grouped3', 'codes3': 'slope9', 'dy12': 'slope3', 'win0': 'slope4'}
+X_CUTS = [(0, 256), (256, 896), (896, 1280)]
+QUEUES = "SSSSASSSSS"
+LOAD_ORDER = [0, 1, 4, 2, 3, 9, 5, 6, 8, 7]
+TAGS = {'dy12': 'slope3', 'xs2': 'th4', 'codes4': 'th9', 'win2': 'grouped1'}
 DB, TB, AB, XB = (4, 1, 2, 1)
-SLOPE_ON = "VVSSVVVGSS"
-DA_ON = "VVVVVVGGGG"
-DYS_CUTS = [(0, 512), (512, 1280)]
-DY_CUTS = [(0, 512), (512, 768), (768, 1280)]
+SLOPE_ON = "SSSSVVVSSS"
+DA_ON = "VVVVGGVVGV"
+DYS_CUTS = [(0, 768), (768, 1280)]
+DY_CUTS = [(0, 512), (512, 896), (896, 1280)]
 SCATTER_CUTS = [(0, 256), (256, 512), (512, 768), (768, 1024), (1024, 1280)]
 
 
@@ -38,8 +40,7 @@ def tile_moe_rec_mlp_silu_kernel(
     nc = tc.nc
     with ExitStack() as ctx:
         held = ctx.enter_context(tc.tile_pool(name="held", bufs=1))
-        work = ctx.enter_context(tc.tile_pool(name="work", bufs=6))
-        psum = ctx.enter_context(tc.psum_pool(name="psum", bufs=2))
+        psum = ctx.enter_context(tc.psum_pool(name="psum", bufs=1))
 
         offsets = held.tile([P, SLOTS // 16], U16, name="offsets")
         nc.sync.dma_start(offsets[:], offs)
@@ -84,27 +85,46 @@ def tile_moe_rec_mlp_silu_kernel(
                     dy_scales[:, 4 * q : 4 * q + 4, :].bitcast(I32),
                 )
 
-        xs_win = load_planes("xs_win", x_scales, nc.scalar)
-        x_win = load_words("x_win", x_words[0])
-        load_codes(w1_codes, w1_words, 0, 2)
-        w1_planes = load_planes("w1_planes", w1_scales.rearrange("e s r n -> (e s) r n"), nc.scalar)
-        nc.sync.dma_start(gate_rows[:], gate.rearrange("r (b p) -> (r b) p", p=P)[0:P, :])
-        load_dys(nc.sync)
+        held_in = {}
         dy_both = held.tile([P, PASSES, T], I32, name="dy_both")
-        nc.sync.dma_start(dy_both[:], dy_words.rearrange("s p t d -> p s (t d)").bitcast(I32))
         dy_win = [dy_both[:, s, :] for s in range(PASSES)]
-        load_codes(w1_codes, w1_words, 2, E)
-        w2_planes = load_planes("w2_planes", w2t_scales.rearrange("e s r n -> (e s) r n"), nc.sync)
-        load_codes(w2_codes, w2t_words, 0, 2)
+
+        def load(what):
+            queue = nc.scalar if QUEUES[what] == "A" else nc.sync
+            if what == 0:
+                held_in["xs"] = load_planes("xs_win", x_scales, queue)
+            elif what == 1:
+                held_in["x"] = load_words("x_win", x_words[0])
+            elif what == 2:
+                load_codes(w1_codes, w1_words, 0, 2)
+            elif what == 3:
+                held_in["w1"] = load_planes("w1_planes", w1_scales.rearrange("e s r n -> (e s) r n"), queue)
+            elif what == 4:
+                queue.dma_start(gate_rows[:], gate.rearrange("r (b p) -> (r b) p", p=P)[0:P, :])
+            elif what == 5:
+                load_dys(queue)
+            elif what == 6:
+                nc.sync.dma_start(dy_both[:], dy_words.rearrange("s p t d -> p s (t d)").bitcast(I32))
+            elif what == 7:
+                load_codes(w1_codes, w1_words, 2, E)
+            elif what == 8:
+                held_in["w2"] = load_planes("w2_planes", w2t_scales.rearrange("e s r n -> (e s) r n"), queue)
+            else:
+                load_codes(w2_codes, w2t_words, 0, 2)
+
+        for what in LOAD_ORDER:
+            load(what)
+        xs_win, x_win, w1_planes, w2_planes = held_in["xs"], held_in["x"], held_in["w1"], held_in["w2"]
 
         ident = held.tile([P, P], F32, name="ident")
-        make_identity(nc, ident[:])
-        gate_ps = psum.tile([P, 2, 2, P], F32, name="turned", tag="turned", bufs=TB)
-        nc.tensor.transpose(gate_ps[:, 0, 0, :], gate_rows[:], ident[:])
-        half_gate = held.tile([P, BLOCKS], F32, name="half_gate")
-        neg_half_gate = held.tile([P, BLOCKS], F32, name="neg_half_gate")
-        nc.scalar.activation(half_gate[:], gate_ps[:, 0, 0, 0:BLOCKS], ACT.Copy, scale=0.5)
-        nc.scalar.activation(neg_half_gate[:], gate_ps[:, 0, 0, 0:BLOCKS], ACT.Copy, scale=-0.5)
+        nc.vector.memset(ident[:], 0.0)
+        make_identity(nc, ident[:], nomemset=True)
+        gate_cols = held.tile([P, BLOCKS], F32, name="gate_cols")
+
+        def turn_gate(unused):
+            gate_ps = psum.tile([P, 2, 2, P], F32, name="turned%d" % (TB - 1))
+            nc.tensor.transpose(gate_ps[:, 0, 0, :], gate_rows[:], ident[:])
+            nc.scalar.copy(gate_cols[:], gate_ps[:, 0, 0, 0:BLOCKS])
 
         def gather(name, window, dtype, cut, tag=""):
             lo, hi = cut
@@ -152,25 +172,22 @@ def tile_moe_rec_mlp_silu_kernel(
         def recompute(block):
             e = block * P // C
             c, cols = cut_of(X_CUTS, block)
-            a_ps = psum.tile([P, H], F32, name="a_ps", bufs=AB)
+            a_ps = psum.tile([P, H], F32, name="a_ps%d" % (block % AB))
             nc.tensor.matmul_mx(
                 out=a_ps[:], lhsT=x_got[c][:, cols].bitcast(FP8X4), lhsT_scale=xs_got[c][:, cols],
                 rhs=w1_codes[:, e, :].bitcast(FP4X4), rhs_scale=w1_planes[:, e, :], start=True, stop=True,
             )
-            neg_silu = work.tile([P, H], F32, name="neg_silu")
+            neg_silu = held.tile([P, H], F32, name="ns%d" % block, tag=TAGS.get("ns%d" % block, ""), align_bytes=64)
             nc.scalar.activation(neg_silu[:], a_ps[:], ACT.Silu, scale=-1.0)
             th = held.tile([P, H], F32, name="th%d" % block, align_bytes=64)
             nc.scalar.activation(th[:], a_ps[:], ACT.Tanh, scale=0.5)
             gated = held.tile([P, H], F32, name="gated%d" % block, align_bytes=64)
-            nc.scalar.activation(
-                gated[:], neg_silu[:], ACT.Identity,
-                bias=half_gate[:, block : block + 1], scale=neg_half_gate[:, block : block + 1],
-            )
+            nc.scalar.activation(gated[:], neg_silu[:], ACT.Identity, bias=0.5, scale=-0.5)
             slope = held.tile([P, H], F32, name="slope%d" % block, align_bytes=64)
             if SLOPE_ON[block] == "V":
                 nc.vector.scalar_tensor_tensor(slope[:], th[:], 1.0, gated[:], ALU.add, ALU.mult)
             else:
-                twice_sg = work.tile([P, H], F32, name="twice_sg")
+                twice_sg = held.tile([P, H], F32, name="twice_sg%d" % block)
                 if SLOPE_ON[block] == "S":
                     nc.scalar.activation(twice_sg[:], th[:], ACT.Identity, bias=1.0)
                 else:
@@ -182,7 +199,7 @@ def tile_moe_rec_mlp_silu_kernel(
             e, b = divmod(block, C // P)
             c, cols = cut_of(DY_CUTS, block)
             cs, scale_cols = cut_of(DYS_CUTS, block)
-            dh_ps = psum.tile([P, H], F32, name="dh_ps", bufs=DB)
+            dh_ps = psum.tile([P, H], F32, name="dh_ps%d" % (block % DB))
             for s in range(PASSES):
                 g = e * PASSES + s
                 nc.tensor.matmul_mx(
@@ -192,14 +209,16 @@ def tile_moe_rec_mlp_silu_kernel(
                 )
             da = held.tile([P, H], BF16, name="da%d" % block)
             if DA_ON[block] == "V":
-                nc.vector.tensor_tensor(da[:], dh_ps[:], slopes[block][:], ALU.mult)
+                nc.vector.scalar_tensor_tensor(
+                    da[:], slopes[block][:], gate_cols[:, block : block + 1], dh_ps[:], ALU.mult, ALU.mult
+                )
             else:
-                dh = work.tile([P, H], F32, name="dh")
-                nc.scalar.copy(dh[:], dh_ps[:])
+                dh = held.tile([P, H], F32, name="dh%d" % block)
+                nc.scalar.activation(dh[:], dh_ps[:], ACT.Copy, scale=gate_cols[:, block : block + 1])
                 nc.gpsimd.tensor_tensor(da[:], dh[:], slopes[block][:], ALU.mult)
             da_words = da[:].bitcast(F32)
             if b == 0:
-                turned[e] = psum.tile([P, 2, 2, P], F32, name="turned", tag="turned", bufs=TB)
+                turned[e] = psum.tile([P, 2, 2, P], F32, name="turned%d" % (e % TB))
             for u in range(2):
                 nc.tensor.transpose(turned[e][:, b, u, :], da_words[:, u : H // 2 : 2], ident[:])
             if b == 1:
@@ -224,7 +243,7 @@ def tile_moe_rec_mlp_silu_kernel(
             da_codes, da_scales = da_mx[e]
             lo = max(start for start in results if start <= e * C)
             for half in range(2):
-                dx_ps = psum.tile([P, 2, C], F32, name="dx_ps", bufs=XB)
+                dx_ps = psum.tile([P, 2, C], F32, name="dx_ps%d" % (half % XB))
                 for j in range(2):
                     kb = 2 * half + j
                     nc.tensor.matmul_mx(
@@ -235,50 +254,53 @@ def tile_moe_rec_mlp_silu_kernel(
                     )
                 nc.scalar.copy(results[lo][:, 2 * half : 2 * half + 2, e * C - lo : (e + 1) * C - lo], dx_ps[:])
 
-        gather_x(0)
-        gather_xs(0)
-        load_late(0)
-        gather_dy(0, 0)
-        gather_dys(0)
-        gather_dy(1, 1)
-        recompute(0)
-        gather_dy(1, 0)
         gather_xs(1)
+        gather_x(0)
+        gather_dy(0, 0)
+        turn_gate(0)
+        gather_dys(0)
+        gather_xs(0)
+        load_late(2)
         gather_x(1)
+        gather_dy(0, 2)
+        recompute(0)
         recompute(1)
+        gather_dy(1, 0)
+        gather_x(2)
         recompute(2)
         hidden_gradient(0)
         hidden_gradient(1)
-        load_late(2)
-        hidden_gradient(2)
-        gather_dy(0, 2)
-        load_late(1)
-        quantise(0)
-        gather_dys(1)
         recompute(3)
+        hidden_gradient(2)
+        gather_dy(1, 1)
+        load_late(1)
         recompute(4)
-        gather_dy(0, 1)
-        hidden_gradient(3)
-        input_gradient(0)
-        quantise(1)
-        hidden_gradient(4)
+        quantise(0)
         recompute(5)
         recompute(6)
-        input_gradient(1)
+        hidden_gradient(3)
+        gather_xs(2)
+        input_gradient(0)
         recompute(7)
-        hidden_gradient(5)
-        recompute(8)
-        recompute(9)
         gather_dy(1, 2)
+        gather_dy(0, 1)
+        gather_dys(1)
+        load_late(0)
+        hidden_gradient(4)
+        quantise(1)
+        recompute(8)
+        hidden_gradient(5)
+        input_gradient(1)
         hidden_gradient(6)
+        quantise(2)
         hidden_gradient(7)
+        input_gradient(2)
+        recompute(9)
+        quantise(3)
         hidden_gradient(8)
         hidden_gradient(9)
-        quantise(3)
-        quantise(2)
-        input_gradient(2)
-        quantise(4)
         input_gradient(3)
+        quantise(4)
         input_gradient(4)
 
         out_win = [

from contextlib import ExitStack

import concourse.mybir as mybir
from concourse.masks import make_identity

K, T, E, C, H, N = 512, 1280, 5, 256, 512, 1024
FLOPS = 2 * E * C * H * (K + N + K)

F32 = mybir.dt.float32
BF16 = mybir.dt.bfloat16
I32 = mybir.dt.int32
U32 = mybir.dt.uint32
U16 = mybir.dt.uint16
U8 = mybir.dt.uint8
FP8X4 = mybir.dt.float8_e4m3fn_x4
FP4X4 = mybir.dt.float4_e2m1fn_x4
ACT = mybir.ActivationFunctionType
ALU = mybir.AluOpType

P = 128
SLOTS = E * C
BLOCKS = SLOTS // P
PASSES = N // 512
X_CUTS = [(0, 256), (256, 896), (896, 1280)]
QUEUES = "SSSSASSSSS"
LOAD_ORDER = [0, 1, 4, 2, 3, 9, 5, 6, 8, 7]
TAGS = {'dy12': 'slope3', 'xs2': 'th4', 'codes4': 'th9', 'win2': 'grouped1'}
DB, TB, AB, XB = (4, 1, 2, 1)
SLOPE_ON = "SSSSVVVSSS"
DA_ON = "VVVVGGVVGV"
DYS_CUTS = [(0, 768), (768, 1280)]
DY_CUTS = [(0, 512), (512, 896), (896, 1280)]
SCATTER_CUTS = [(0, 256), (256, 512), (512, 768), (768, 1024), (1024, 1280)]


def tile_moe_rec_mlp_silu_kernel(
    tc, x_words, x_scales, dy_words, dy_scales, w1_words, w1_scales, w2t_words, w2t_scales,
    w1t_words, w1t_scales, gate, offs, out,
):
    nc = tc.nc
    with ExitStack() as ctx:
        held = ctx.enter_context(tc.tile_pool(name="held", bufs=1))
        psum = ctx.enter_context(tc.psum_pool(name="psum", bufs=1))

        offsets = held.tile([P, SLOTS // 16], U16, name="offsets")
        nc.sync.dma_start(offsets[:], offs)

        def listed(lo, hi):
            return offsets[:, lo // 16 : hi // 16]

        def load_words(name, words):
            win = held.tile([P, T], I32, name=name)
            nc.sync.dma_start(win[:], words.rearrange("p t d -> p (t d)").bitcast(I32))
            return win

        def load_planes(name, scales, queue):
            groups, width = scales.shape[0], scales.shape[2]
            planes = held.tile([P, groups, width], U8, name=name, align_bytes=64)
            nc.vector.memset(planes[:].rearrange("p g n -> p (g n)").bitcast(I32), 0)
            for q in range(4):
                queue.dma_start(
                    planes[32 * q : 32 * q + 4, :, :].bitcast(I32),
                    scales[:, 4 * q : 4 * q + 4, :].rearrange("g r n -> r g n").bitcast(I32),
                )
            return planes

        def load_codes(codes, words, e0, e1):
            per = words.shape[1]
            nc.sync.dma_start(
                codes[:, e0 * per : e1 * per, :].bitcast(I32),
                words[e0:e1].rearrange("e s p n -> p (e s) n").bitcast(I32),
            )

        w1_codes = held.tile([P, E, 2 * H], U8, name="w1_codes", align_bytes=64)
        w2_codes = held.tile([P, E * PASSES, 2 * H], U8, name="w2_codes", align_bytes=64)
        w1t_codes = held.tile([P, E, 2 * K], U8, name="w1t_codes", align_bytes=64)
        gate_rows = held.tile([P, P], F32, name="gate_rows")
        dys_win = held.tile([P, T], U8, name="dys_win", align_bytes=64)

        def load_dys(queue):
            nc.vector.memset(dys_win[:].bitcast(I32), 0)
            for q in range(4):
                queue.dma_start(
                    dys_win[32 * q : 32 * q + 4 * PASSES, :].bitcast(I32),
                    dy_scales[:, 4 * q : 4 * q + 4, :].bitcast(I32),
                )

        held_in = {}
        dy_both = held.tile([P, PASSES, T], I32, name="dy_both")
        dy_win = [dy_both[:, s, :] for s in range(PASSES)]

        def load(what):
            queue = nc.scalar if QUEUES[what] == "A" else nc.sync
            if what == 0:
                held_in["xs"] = load_planes("xs_win", x_scales, queue)
            elif what == 1:
                held_in["x"] = load_words("x_win", x_words[0])
            elif what == 2:
                load_codes(w1_codes, w1_words, 0, 2)
            elif what == 3:
                held_in["w1"] = load_planes("w1_planes", w1_scales.rearrange("e s r n -> (e s) r n"), queue)
            elif what == 4:
                queue.dma_start(gate_rows[:], gate.rearrange("r (b p) -> (r b) p", p=P)[0:P, :])
            elif what == 5:
                load_dys(queue)
            elif what == 6:
                nc.sync.dma_start(dy_both[:], dy_words.rearrange("s p t d -> p s (t d)").bitcast(I32))
            elif what == 7:
                load_codes(w1_codes, w1_words, 2, E)
            elif what == 8:
                held_in["w2"] = load_planes("w2_planes", w2t_scales.rearrange("e s r n -> (e s) r n"), queue)
            else:
                load_codes(w2_codes, w2t_words, 0, 2)

        for what in LOAD_ORDER:
            load(what)
        xs_win, x_win, w1_planes, w2_planes = held_in["xs"], held_in["x"], held_in["w1"], held_in["w2"]

        ident = held.tile([P, P], F32, name="ident")
        nc.vector.memset(ident[:], 0.0)
        make_identity(nc, ident[:], nomemset=True)
        gate_cols = held.tile([P, BLOCKS], F32, name="gate_cols")

        def turn_gate(unused):
            gate_ps = psum.tile([P, 2, 2, P], F32, name="turned%d" % (TB - 1))
            nc.tensor.transpose(gate_ps[:, 0, 0, :], gate_rows[:], ident[:])
            nc.scalar.copy(gate_cols[:], gate_ps[:, 0, 0, 0:BLOCKS])

        def gather(name, window, dtype, cut, tag=""):
            lo, hi = cut
            got = held.tile([P, hi - lo], dtype, name="%s_%d" % (name, lo), tag=tag, align_bytes=64)
            nc.vector.tensor_copy(got[:], window.indirect(listed(lo, hi)))
            return got

        def cut_of(cuts, block):
            c = max(i for i, cut in enumerate(cuts) if cut[0] <= block * P)
            lo = cuts[c][0]
            return c, slice(block * P - lo, (block + 1) * P - lo)

        x_got, xs_got, dy_got, dys_got = {}, {}, [{}, {}], {}

        def gather_x(c):
            x_got[c] = gather("x_got", x_win[:].bitcast(U32), U32, X_CUTS[c], TAGS.get("x%d" % c, ""))

        def gather_xs(c):
            xs_got[c] = gather("xs_got", xs_win[:, 0, :], U8, X_CUTS[c], TAGS.get("xs%d" % c, ""))

        def gather_dys(c):
            cut = DYS_CUTS[c]
            both = gather("dys_got", dys_win[:], U8, cut, TAGS.get("dys%d" % c, ""))
            moved = held.tile([P, cut[1] - cut[0]], U8, name="dys_moved%d" % cut[0], align_bytes=64)
            nc.vector.memset(moved[:].bitcast(I32), 0)
            nc.sync.dma_start(moved[0:112, :].bitcast(I32), both[4:116, :].bitcast(I32))
            dys_got[c] = [both, moved]

        def gather_dy(s, c):
            cut = DY_CUTS[c]
            dy_got[s][cut[0]] = gather("dy_got%d" % s, dy_win[s][:].bitcast(U32), U32, cut, TAGS.get("dy%d%d" % (s, c), ""))

        late = {}

        def load_late(what):
            if what == 0:
                load_codes(w2_codes, w2t_words, 2, E)
            elif what == 1:
                late["w1t_planes"] = load_planes("w1t_planes", w1t_scales.rearrange("e s r n -> (e s) r n"), nc.sync)
            else:
                load_codes(w1t_codes, w1t_words, 0, E)

        slopes, grouped, da_mx, turned = {}, {}, {}, {}

        def recompute(block):
            e = block * P // C
            c, cols = cut_of(X_CUTS, block)
            a_ps = psum.tile([P, H], F32, name="a_ps%d" % (block % AB))
            nc.tensor.matmul_mx(
                out=a_ps[:], lhsT=x_got[c][:, cols].bitcast(FP8X4), lhsT_scale=xs_got[c][:, cols],
                rhs=w1_codes[:, e, :].bitcast(FP4X4), rhs_scale=w1_planes[:, e, :], start=True, stop=True,
            )
            neg_silu = held.tile([P, H], F32, name="ns%d" % block, tag=TAGS.get("ns%d" % block, ""), align_bytes=64)
            nc.scalar.activation(neg_silu[:], a_ps[:], ACT.Silu, scale=-1.0)
            th = held.tile([P, H], F32, name="th%d" % block, align_bytes=64)
            nc.scalar.activation(th[:], a_ps[:], ACT.Tanh, scale=0.5)
            gated = held.tile([P, H], F32, name="gated%d" % block, align_bytes=64)
            nc.scalar.activation(gated[:], neg_silu[:], ACT.Identity, bias=0.5, scale=-0.5)
            slope = held.tile([P, H], F32, name="slope%d" % block, align_bytes=64)
            if SLOPE_ON[block] == "V":
                nc.vector.scalar_tensor_tensor(slope[:], th[:], 1.0, gated[:], ALU.add, ALU.mult)
            else:
                twice_sg = held.tile([P, H], F32, name="twice_sg%d" % block)
                if SLOPE_ON[block] == "S":
                    nc.scalar.activation(twice_sg[:], th[:], ACT.Identity, bias=1.0)
                else:
                    nc.gpsimd.tensor_scalar(twice_sg[:], th[:], 1.0, 1.0, ALU.mult, ALU.add)
                nc.gpsimd.tensor_tensor(slope[:], twice_sg[:], gated[:], ALU.mult)
            slopes[block] = slope

        def hidden_gradient(block):
            e, b = divmod(block, C // P)
            c, cols = cut_of(DY_CUTS, block)
            cs, scale_cols = cut_of(DYS_CUTS, block)
            dh_ps = psum.tile([P, H], F32, name="dh_ps%d" % (block % DB))
            for s in range(PASSES):
                g = e * PASSES + s
                nc.tensor.matmul_mx(
                    out=dh_ps[:], lhsT=dy_got[s][DY_CUTS[c][0]][:, cols].bitcast(FP8X4), lhsT_scale=dys_got[cs][s][:, scale_cols],
                    rhs=w2_codes[:, g, :].bitcast(FP4X4), rhs_scale=w2_planes[:, g, :],
                    start=(s == 0), stop=(s == PASSES - 1),
                )
            da = held.tile([P, H], BF16, name="da%d" % block)
            if DA_ON[block] == "V":
                nc.vector.scalar_tensor_tensor(
                    da[:], slopes[block][:], gate_cols[:, block : block + 1], dh_ps[:], ALU.mult, ALU.mult
                )
            else:
                dh = held.tile([P, H], F32, name="dh%d" % block)
                nc.scalar.activation(dh[:], dh_ps[:], ACT.Copy, scale=gate_cols[:, block : block + 1])
                nc.gpsimd.tensor_tensor(da[:], dh[:], slopes[block][:], ALU.mult)
            da_words = da[:].bitcast(F32)
            if b == 0:
                turned[e] = psum.tile([P, 2, 2, P], F32, name="turned%d" % (e % TB))
            for u in range(2):
                nc.tensor.transpose(turned[e][:, b, u, :], da_words[:, u : H // 2 : 2], ident[:])
            if b == 1:
                grouped[e] = held.tile([P, 4 * C], BF16, name="grouped%d" % e, align_bytes=64)
                nc.scalar.copy(
                    grouped[e][:].bitcast(F32).rearrange("p (b r u) -> p b r u", b=2, u=2),
                    turned[e][:].rearrange("p b u r -> p b r u"),
                )

        def quantise(e):
            tag = TAGS.get("codes%d" % e, "codes%d" % e)
            da_codes = held.tile([P, C], U32, name="da_codes%d" % e, tag=tag, align_bytes=64)
            da_scales = held.tile([P, C], U8, name="da_scales%d" % e, align_bytes=64)
            nc.vector.quantize_mx(out=da_codes[:].bitcast(FP8X4), scales=da_scales[:], in_=grouped[e][:])
            da_mx[e] = (da_codes, da_scales)

        results = {}
        for lo, hi in SCATTER_CUTS:
            results[lo] = held.tile([P, K // P, hi - lo], F32, name="dx_%d" % lo)

        def input_gradient(e):
            da_codes, da_scales = da_mx[e]
            lo = max(start for start in results if start <= e * C)
            for half in range(2):
                dx_ps = psum.tile([P, 2, C], F32, name="dx_ps%d" % (half % XB))
                for j in range(2):
                    kb = 2 * half + j
                    nc.tensor.matmul_mx(
                        out=dx_ps[:, j, :],
                        lhsT=w1t_codes[:, e, 2 * P * kb : 2 * P * (kb + 1)].bitcast(FP4X4),
                        lhsT_scale=late["w1t_planes"][:, e, P * kb : P * (kb + 1)],
                        rhs=da_codes[:].bitcast(FP8X4), rhs_scale=da_scales[:], start=True, stop=True,
                    )
                nc.scalar.copy(results[lo][:, 2 * half : 2 * half + 2, e * C - lo : (e + 1) * C - lo], dx_ps[:])

        gather_xs(1)
        gather_x(0)
        gather_dy(0, 0)
        turn_gate(0)
        gather_dys(0)
        gather_xs(0)
        load_late(2)
        gather_x(1)
        gather_dy(0, 2)
        recompute(0)
        recompute(1)
        gather_dy(1, 0)
        gather_x(2)
        recompute(2)
        hidden_gradient(0)
        hidden_gradient(1)
        recompute(3)
        hidden_gradient(2)
        gather_dy(1, 1)
        load_late(1)
        recompute(4)
        quantise(0)
        recompute(5)
        recompute(6)
        hidden_gradient(3)
        gather_xs(2)
        input_gradient(0)
        recompute(7)
        gather_dy(1, 2)
        gather_dy(0, 1)
        gather_dys(1)
        load_late(0)
        hidden_gradient(4)
        quantise(1)
        recompute(8)
        hidden_gradient(5)
        input_gradient(1)
        hidden_gradient(6)
        quantise(2)
        hidden_gradient(7)
        input_gradient(2)
        recompute(9)
        quantise(3)
        hidden_gradient(8)
        hidden_gradient(9)
        input_gradient(3)
        quantise(4)
        input_gradient(4)

        out_win = [
            held.tile([P, T], F32, name="out_win%d" % kb, tag=TAGS.get("win%d" % kb, "win%d" % kb), align_bytes=64) for kb in range(K // P)
        ]
        for lo, hi in SCATTER_CUTS:
            for kb in range(K // P):
                nc.vector.tensor_copy(out_win[kb][:].indirect(listed(lo, hi)), results[lo][:, kb, :])
        for kb in range(K // P):
            nc.sync.dma_start(out[kb * P : (kb + 1) * P, :], out_win[kb][:])
